import numpy as np
import ml_dtypes


def mxq(x, axis, fmt="e4m3"):
    dtype, down = {"e4m3": (ml_dtypes.float8_e4m3fn, 7), "e5m2": (ml_dtypes.float8_e5m2, 14)}[fmt]
    v = np.moveaxis(np.asarray(x, np.float32).astype(ml_dtypes.bfloat16).astype(np.float64), axis, -1)
    blocks = v.reshape(v.shape[:-1] + (-1, 32))
    amax = np.abs(blocks).max(-1, keepdims=True)
    byte = np.maximum(np.where(amax > 0, np.frexp(amax)[1] - 1 + 127, 0) - down, 1)
    scale = np.exp2(byte - 127.0)
    codes = (blocks / scale).astype(np.float32).astype(dtype).astype(np.float64)
    return np.moveaxis((codes * scale).reshape(v.shape), -1, axis)


WIDE = False


def mx_kscale(k):
    if not WIDE:
        return np.ones(k)
    levels = np.array([10, -10, 5, -5, 0])
    if k % 512:
        return np.exp2(np.random.permutation(np.resize(levels, k // 32))).repeat(32)
    a = np.empty((k // 512, 16))
    for p in range(k // 512):
        a[p, :8] = np.random.permutation(np.resize(levels, 8))
        for g in range(8):
            far = levels[np.abs(levels - a[p, g]) >= 10]
            a[p, g + 8] = far[np.random.randint(len(far))]
    return np.exp2(a.ravel()).repeat(32)


def f64(x):
    return np.asarray(x).astype(np.float64)


def striped(idx):
    return np.tile(idx.reshape(-1, 16).T, (8, 1)).astype(np.uint16)


def unstriped(offs):
    return offs[:16].T.reshape(-1).astype(np.int64)


def striped8(idx):
    return np.concatenate([x.reshape(-1, 16).T for x in idx]).astype(np.uint16)


def runs(offs, k):
    lists = np.stack([offs[16 * r : 16 * r + 16].T.reshape(-1) for r in range(8)]).astype(np.int64)
    return lists[np.arange(k) % 512 // 64]


def pack_weight(w):
    k, n = w.shape
    w = f64(np.asarray(w, np.float32).astype(ml_dtypes.bfloat16)).reshape(k // 32, 32, n)
    amax = np.abs(w).max(1)
    byte = np.clip(np.where(amax > 0, np.frexp(amax)[1] - 1 + 127 - 7, 1), 1, 254)
    scaled = (w * np.exp2(127.0 - byte)[:, None, :]).reshape(k, n).astype(np.float32)
    words = np.ascontiguousarray(scaled.reshape(k // 512, 128, 4, n).transpose(0, 1, 3, 2)).astype(ml_dtypes.float8_e4m3fn).view(np.uint8)
    return words, np.ascontiguousarray(byte.astype(np.uint8).reshape(k // 512, 16, n))


def unpack_weight(words, scales):
    g, p, n, _ = words.shape
    vals = np.ascontiguousarray(words).view(ml_dtypes.float8_e4m3fn).astype(np.float64) * np.repeat(np.exp2(scales.astype(np.float64) - 127.0), 8, axis=1)[..., None]
    return vals.transpose(0, 1, 3, 2).reshape(g * 512, n)


def relu(v):
    return np.maximum(v, 0.0)


K, T, S, N, H = 512, 2048, 512, 512, 512


def setup_inputs():
    n = np.random.standard_normal
    s = mx_kscale(K)[:, None]
    u = mx_kscale(H)
    packed_xT = pack_weight(n((K, T)) * s)
    return {
        "x_words": packed_xT[0],
        "x_scales": packed_xT[1],
        "w1": (n((K, H)) / np.sqrt(K) / s).astype(np.float32),
        "gn": (np.random.uniform(0.5, 1.5, (H, 1)) * u[:, None]).astype(np.float32),
        "w2": (n((H, N)) / np.sqrt(H) / u[:, None]).astype(np.float32),
        "offs": striped(np.random.permutation(T)[:S]),
        "n1": striped8(np.stack([np.random.permutation(S) for _ in range(8)])),
        "n2": striped8(np.stack([np.random.permutation(S) for _ in range(8)])),
        "n3": striped8(np.stack([np.random.permutation(S) for _ in range(8)])),
        "n4": striped8(np.stack([np.random.permutation(S) for _ in range(8)])),
    }


def reference(x_words, x_scales, w1, gn, w2, offs, n1, n2, n3, n4):
    xq = unpack_weight(x_words, x_scales)[:, unstriped(offs)]
    y = mxq(f64(w1), 0, "e4m3").T @ xq
    a = y[np.arange(H)[:, None], runs(n1, H)]
    b = y[np.arange(H)[:, None], runs(n2, H)]
    c = y[np.arange(H)[:, None], runs(n3, H)]
    z = f64(gn) * (np.maximum(np.maximum(a, b), c) - (0.5 * (np.minimum(np.minimum(a, b), c))))
    h = mxq(f64(w2), 0, "e4m3").T @ mxq(z, 0, "e4m3")
    return h + -0.5 * (relu(h[np.arange(N)[:, None], runs(n4, N)]))

@@ -1,0 +1,200 @@
+from contextlib import ExitStack
+
+import concourse.mybir as mybir
+
+K, T, S, N, H = 512, 2048, 512, 512, 512
+FLOPS = 2 * K * H * S + 2 * H * N * S
+
+F32 = mybir.dt.float32
+BF16 = mybir.dt.bfloat16
+I32 = mybir.dt.int32
+U32 = mybir.dt.uint32
+U16 = mybir.dt.uint16
+U8 = mybir.dt.uint8
+FP8X4 = mybir.dt.float8_e4m3fn_x4
+ALU = mybir.AluOpType
+ACT = mybir.ActivationFunctionType
+
+P = 128
+PACK = 4
+LIST_ROWS = 16
+HALF = S // 2
+CHUNKS = ((0, 256), (256, 128), (384, 128))
+
+
+def entries(list_tile, start, count):
+    return list_tile[:, start // LIST_ROWS : (start + count) // LIST_ROWS]
+
+
+def deal_columns(copy, dealt, raw, m0, m1):
+    copy(
+        out=dealt[:, :, m0:m1, :].rearrange("p t m j -> p m j t"),
+        in_=raw[:].rearrange("p j (m t) -> p m j t", t=PACK)[:, m0:m1, :, :],
+    )
+
+
+def tile_picked_rangelay_none_p_kernel(tc, x_words, x_scales, w1, gn, w2, offs, n1, n2, n3, n4, out):
+    nc = tc.nc
+    with ExitStack() as ctx:
+        keep = ctx.enter_context(tc.tile_pool(name="keep", bufs=1))
+        psum = ctx.enter_context(tc.psum_pool(name="psum", bufs=8))
+
+        lists = {}
+        for name in ("offs", "n1", "n2", "n3", "n4"):
+            lists[name] = keep.tile([P, S // LIST_ROWS], U16, name="list_" + name)
+        all_words = keep.tile([P, T], U32, align_bytes=64)
+        all_scales = keep.tile([P, T], U8, align_bytes=64)
+        w1_raw = keep.tile([P, PACK, H], F32, align_bytes=64)
+        w2_raw = keep.tile([P, PACK, N], F32, align_bytes=64)
+        gain = keep.tile([P, PACK], F32)
+
+        nc.vector.memset(all_scales[:].bitcast(I32), 0)
+        nc.sync.dma_start(lists["offs"][:], offs)
+        for q in range(4):
+            nc.scalar.dma_start(
+                out=all_scales[32 * q : 32 * q + 4, :].bitcast(I32), in_=x_scales[0, 4 * q : 4 * q + 4, :].bitcast(I32)
+            )
+        nc.scalar.dma_start(out=gain[:], in_=gn.rearrange("(p t) o -> p (t o)", t=PACK))
+        nc.sync.dma_start(out=w1_raw[:], in_=w1.rearrange("(p j) c -> p j c", j=PACK))
+        nc.sync.dma_start(out=all_words[:].bitcast(I32), in_=x_words[0].rearrange("p n t -> p (n t)").bitcast(I32))
+        nc.sync.dma_start(lists["n1"][:], n1)
+        nc.sync.dma_start(lists["n2"][:], n2)
+        nc.sync.dma_start(lists["n3"][:], n3)
+        nc.sync.dma_start(out=w2_raw[:], in_=w2.rearrange("(p j) c -> p j c", j=PACK))
+        nc.sync.dma_start(lists["n4"][:], n4)
+
+        half_gain = keep.tile([P, PACK], F32)
+        not_negative = keep.tile([P, PACK], F32)
+        min_share = keep.tile([P, PACK], F32)
+        range_factor = keep.tile([P, PACK], F32)
+        nc.vector.tensor_scalar(not_negative[:], gain[:], 0.0, None, ALU.is_ge)
+        nc.vector.tensor_scalar(half_gain[:], gain[:], 0.5, None, ALU.mult)
+        x_scale = keep.tile([P, S], U8, align_bytes=64)
+        nc.vector.tensor_copy(x_scale[:], all_scales[:].indirect(lists["offs"][:]))
+        nc.vector.tensor_scalar(min_share[:], not_negative[:], 1.5, -2.0, ALU.mult, ALU.add)
+        nc.vector.tensor_scalar(range_factor[:], not_negative[:], 3.0, -1.0, ALU.mult, ALU.add)
+
+        w1_dealt = keep.tile([P, PACK, P, PACK], BF16, align_bytes=64)
+        w1_codes = keep.tile([P, H], U32, align_bytes=64)
+        w1_scale = keep.tile([P, H], U8, align_bytes=64)
+        deal_columns(nc.scalar.copy, w1_dealt, w1_raw, 0, 48)
+        deal_columns(nc.vector.tensor_copy, w1_dealt, w1_raw, 48, P)
+        nc.vector.quantize_mx(w1_codes[:].bitcast(FP8X4), w1_scale[:], w1_dealt[:].rearrange("p t m j -> p (t m j)"))
+
+        x_codes = keep.tile([P, S], U32, align_bytes=64)
+        for j0 in (0, HALF):
+            nc.vector.tensor_copy(x_codes[:, j0 : j0 + HALF], all_words[:].indirect(entries(lists["offs"], j0, HALF)))
+
+        y_rows = [keep.tile([P, S], F32, name="y_rows%d" % t, align_bytes=64) for t in range(PACK)]
+        for t in range(PACK):
+            rows = slice(t * P, (t + 1) * P)
+            for j0, n in ((0, HALF), (HALF, HALF)) if t == 0 else ((0, S),):
+                bank = psum.tile([P, S], F32, name="bank")
+                nc.tensor.matmul_mx(
+                    out=bank[:, :n],
+                    lhsT=w1_codes[:, rows].bitcast(FP8X4),
+                    lhsT_scale=w1_scale[:, rows],
+                    rhs=x_codes[:, j0 : j0 + n].bitcast(FP8X4),
+                    rhs_scale=x_scale[:, j0 : j0 + n],
+                    start=True,
+                    stop=True,
+                )
+                nc.scalar.activation(y_rows[t][:, j0 : j0 + n], bank[:, :n], ACT.Copy, scale=half_gain[:, t : t + 1])
+
+        w2_dealt = keep.tile([P, PACK, P, PACK], BF16, align_bytes=64)
+        w2_codes = keep.tile([P, N], U32, align_bytes=64)
+        w2_scale = keep.tile([P, N], U8, align_bytes=64)
+        deal_columns(nc.scalar.copy, w2_dealt, w2_raw, 0, P)
+
+        h_rows = [keep.tile([P, S], F32, name="h_rows%d" % t, align_bytes=64) for t in range(PACK)]
+        penalty = [keep.tile([P, S], F32, name="penalty%d" % t, align_bytes=64) for t in range(PACK)]
+        positive = [keep.tile([P, S], F32, name="positive%d" % t, align_bytes=64) for t in range(PACK)]
+
+        work = {}
+        for c, (j0, n) in enumerate(CHUNKS):
+            for name in ("a", "db", "dc", "hi", "lo"):
+                for t in range(PACK):
+                    work[name, c, t] = keep.tile([P, n], F32, name="%s_%d_%d" % (name, c, t), align_bytes=64)
+            work["z", c] = keep.tile([P, PACK, n], F32, name="z_%d" % c, align_bytes=64)
+            work["zb", c] = keep.tile([P, n, PACK], BF16, name="zb_%d" % c, align_bytes=64)
+            work["zc", c] = keep.tile([P, n], U32, name="zc_%d" % c, align_bytes=64)
+            work["zs", c] = keep.tile([P, n], U8, name="zs_%d" % c, align_bytes=64)
+
+        def fetch_first(c, t):
+            j0, n = CHUNKS[c]
+            nc.vector.tensor_copy(work["a", c, t][:], y_rows[t][:].indirect(entries(lists["n1"], j0, n)))
+
+        def fetch_differences(c, t):
+            j0, n = CHUNKS[c]
+            for name, which in (("db", "n2"), ("dc", "n3")):
+                nc.vector.tensor_tensor(
+                    work[name, c, t][:], y_rows[t][:].indirect(entries(lists[which], j0, n)), work["a", c, t][:], ALU.subtract
+                )
+
+        def extremes(c, t):
+            for name, op in (("hi", ALU.max), ("lo", ALU.min)):
+                nc.vector.scalar_tensor_tensor(work[name, c, t][:], work["db", c, t][:], 0.0, work["dc", c, t][:], op, op)
+
+        def spread(c, t):
+            nc.vector.scalar_tensor_tensor(
+                work["db", c, t][:], work["lo", c, t][:], min_share[:, t : t + 1], work["hi", c, t][:], ALU.mult, ALU.add
+            )
+
+        def finish_z(c, t):
+            nc.vector.scalar_tensor_tensor(
+                work["z", c][:, t, :], work["db", c, t][:], range_factor[:, t : t + 1], work["a", c, t][:], ALU.mult, ALU.add
+            )
+            if t == PACK - 1:
+                nc.scalar.copy(
+                    out=work["zb", c][:].rearrange("p (g i) t -> p g t i", i=4),
+                    in_=work["z", c][:].rearrange("p t (g i) -> p g t i", i=4),
+                )
+
+        def second_product(c, t):
+            if c == 0 and t == 0:
+                nc.vector.quantize_mx(w2_codes[:].bitcast(FP8X4), w2_scale[:], w2_dealt[:].rearrange("p t m j -> p (t m j)"))
+            if t != PACK - 1:
+                return
+            j0, n = CHUNKS[c]
+            last = c == len(CHUNKS) - 1
+            nc.vector.quantize_mx(work["zc", c][:].bitcast(FP8X4), work["zs", c][:], work["zb", c][:].rearrange("p n t -> p (n t)"))
+            for u in range(PACK):
+                rows = slice(u * P, (u + 1) * P)
+                bank = psum.tile([P, S], F32, name="bank")
+                nc.tensor.matmul_mx(
+                    out=bank[:, :n],
+                    lhsT=w2_codes[:, rows].bitcast(FP8X4),
+                    lhsT_scale=w2_scale[:, rows],
+                    rhs=work["zc", c][:].bitcast(FP8X4),
+                    rhs_scale=work["zs", c][:],
+                    start=True,
+                    stop=True,
+                )
+                cols = slice(j0, j0 + n)
+                if last and u == 0:
+                    nc.vector.tensor_scalar(penalty[u][:, cols], bank[:, :n], -0.5, 0.0, ALU.mult, ALU.min)
+                    nc.scalar.copy(h_rows[u][:, cols], bank[:, :n])
+                else:
+                    nc.scalar.activation(positive[u][:, cols], bank[:, :n], ACT.Relu, scale=0.5)
+                    nc.scalar.copy(h_rows[u][:, cols], bank[:, :n])
+                    nc.scalar.mul(penalty[u][:, cols], positive[u][:, cols], -1.0)
+
+        units = [(c, t) for c in range(len(CHUNKS)) for t in range(PACK)]
+        stages = (fetch_first, fetch_differences, extremes, spread, finish_z, second_product)
+        for step in range(len(units) + len(stages) - 1):
+            for lag, stage in enumerate(stages):
+                if 0 <= step - lag < len(units):
+                    stage(*units[step - lag])
+
+        out_rows = out.rearrange("(p t) s -> p t s", t=PACK)
+        for u in range(PACK):
+            result = keep.tile([P, S], F32, name="result%d" % u, align_bytes=64)
+            for j0 in (0, HALF):
+                cols = slice(j0, j0 + HALF)
+                nc.vector.tensor_tensor(
+                    result[:, cols], penalty[u][:].indirect(entries(lists["n4"], j0, HALF)), h_rows[u][:, cols], ALU.add
+                )
+                if u == PACK - 1:
+                    nc.sync.dma_start(out=out_rows[:, u, cols], in_=result[:, cols])
+            if u < PACK - 1:
+                nc.sync.dma_start(out=out_rows[:, u, :], in_=result[:])

@@ -1,6 +1,7 @@
 from contextlib import ExitStack
 
 import concourse.mybir as mybir
+from concourse.masks import make_identity
 
 K, T, S, N, H = 512, 2048, 512, 512, 512
 FLOPS = 2 * K * H * S + 2 * H * N * S
@@ -19,7 +20,9 @@ P = 128
 PACK = 4
 LIST_ROWS = 16
 HALF = S // 2
-CHUNKS = ((0, 256), (256, 128), (384, 128))
+BLOCK = 128
+BLOCKS = S // BLOCK
+LAST = BLOCKS - 1
 
 
 def entries(list_tile, start, count):
@@ -29,7 +32,7 @@ def entries(list_tile, start, count):
 def deal_columns(copy, dealt, raw, m0, m1):
     copy(
         out=dealt[:, :, m0:m1, :].rearrange("p t m j -> p m j t"),
-        in_=raw[:].rearrange("p j (m t) -> p m j t", t=PACK)[:, m0:m1, :, :],
+        in_=raw[:].rearrange("p j (m t) -> p m j t", t=PACK),
     )
 
 
@@ -44,18 +47,20 @@ def tile_picked_rangelay_none_p_kernel(tc, x_words, x_scales, w1, gn, w2, offs, 
             lists[name] = keep.tile([P, S // LIST_ROWS], U16, name="list_" + name)
         all_words = keep.tile([P, T], U32, align_bytes=64)
         all_scales = keep.tile([P, T], U8, align_bytes=64)
-        w1_raw = keep.tile([P, PACK, H], F32, align_bytes=64)
+        w1_raw = [keep.tile([P, PACK, H // 2], F32, name="w1_raw%d" % i, align_bytes=64) for i in range(2)]
+        w1_rows = w1.rearrange("(p j) c -> p j c", j=PACK)
         w2_raw = keep.tile([P, PACK, N], F32, align_bytes=64)
         gain = keep.tile([P, PACK], F32)
 
         nc.vector.memset(all_scales[:].bitcast(I32), 0)
-        nc.sync.dma_start(lists["offs"][:], offs)
+        nc.scalar.dma_start(out=gain[:], in_=gn.rearrange("(p t) o -> p (t o)", t=PACK))
+        nc.sync.dma_start(out=w1_raw[0][:], in_=w1_rows[:, :, : H // 2])
         for q in range(4):
-            nc.scalar.dma_start(
+            nc.sync.dma_start(
                 out=all_scales[32 * q : 32 * q + 4, :].bitcast(I32), in_=x_scales[0, 4 * q : 4 * q + 4, :].bitcast(I32)
             )
-        nc.scalar.dma_start(out=gain[:], in_=gn.rearrange("(p t) o -> p (t o)", t=PACK))
-        nc.sync.dma_start(out=w1_raw[:], in_=w1.rearrange("(p j) c -> p j c", j=PACK))
+        nc.sync.dma_start(lists["offs"][:], offs)
+        nc.sync.dma_start(out=w1_raw[1][:], in_=w1_rows[:, :, H // 2 :])
         nc.sync.dma_start(out=all_words[:].bitcast(I32), in_=x_words[0].rearrange("p n t -> p (n t)").bitcast(I32))
         nc.sync.dma_start(lists["n1"][:], n1)
         nc.sync.dma_start(lists["n2"][:], n2)
@@ -63,42 +68,49 @@ def tile_picked_rangelay_none_p_kernel(tc, x_words, x_scales, w1, gn, w2, offs, 
         nc.sync.dma_start(out=w2_raw[:], in_=w2.rearrange("(p j) c -> p j c", j=PACK))
         nc.sync.dma_start(lists["n4"][:], n4)
 
+        identity = keep.tile([P, P], F32, align_bytes=64)
+        make_identity(nc, identity[:])
+
         half_gain = keep.tile([P, PACK], F32)
         not_negative = keep.tile([P, PACK], F32)
-        min_share = keep.tile([P, PACK], F32)
-        range_factor = keep.tile([P, PACK], F32)
+        hi_factor = keep.tile([P, PACK], F32)
+        lo_factor = keep.tile([P, PACK], F32)
+        lo_share = keep.tile([P, PACK], F32)
         nc.vector.tensor_scalar(not_negative[:], gain[:], 0.0, None, ALU.is_ge)
-        nc.vector.tensor_scalar(half_gain[:], gain[:], 0.5, None, ALU.mult)
+        nc.scalar.activation(half_gain[:], gain[:], ACT.Copy, scale=0.5)
         x_scale = keep.tile([P, S], U8, align_bytes=64)
         nc.vector.tensor_copy(x_scale[:], all_scales[:].indirect(lists["offs"][:]))
-        nc.vector.tensor_scalar(min_share[:], not_negative[:], 1.5, -2.0, ALU.mult, ALU.add)
-        nc.vector.tensor_scalar(range_factor[:], not_negative[:], 3.0, -1.0, ALU.mult, ALU.add)
+        nc.vector.tensor_scalar(hi_factor[:], not_negative[:], 3.0, -1.0, ALU.mult, ALU.add)
+        nc.vector.tensor_scalar(lo_factor[:], not_negative[:], -3.0, 2.0, ALU.mult, ALU.add)
+        nc.vector.tensor_scalar(lo_share[:], not_negative[:], 1.5, -2.0, ALU.mult, ALU.add)
 
         w1_dealt = keep.tile([P, PACK, P, PACK], BF16, align_bytes=64)
         w1_codes = keep.tile([P, H], U32, align_bytes=64)
         w1_scale = keep.tile([P, H], U8, align_bytes=64)
-        deal_columns(nc.scalar.copy, w1_dealt, w1_raw, 0, 48)
-        deal_columns(nc.vector.tensor_copy, w1_dealt, w1_raw, 48, P)
+        deal_columns(nc.scalar.copy, w1_dealt, w1_raw[0], 0, 64)
+        deal_columns(nc.vector.tensor_copy, w1_dealt, w1_raw[1], 64, P)
         nc.vector.quantize_mx(w1_codes[:].bitcast(FP8X4), w1_scale[:], w1_dealt[:].rearrange("p t m j -> p (t m j)"))
 
         x_codes = keep.tile([P, S], U32, align_bytes=64)
         for j0 in (0, HALF):
             nc.vector.tensor_copy(x_codes[:, j0 : j0 + HALF], all_words[:].indirect(entries(lists["offs"], j0, HALF)))
 
+        def product(bank_cols, codes, scale, rows, moving_codes, moving_scale):
+            nc.tensor.matmul_mx(
+                out=bank_cols,
+                lhsT=codes[:, rows * P : (rows + 1) * P].bitcast(FP8X4),
+                lhsT_scale=scale[:, rows * P : (rows + 1) * P],
+                rhs=moving_codes.bitcast(FP8X4),
+                rhs_scale=moving_scale,
+                start=True,
+                stop=True,
+            )
+
         y_rows = [keep.tile([P, S], F32, name="y_rows%d" % t, align_bytes=64) for t in range(PACK)]
         for t in range(PACK):
-            rows = slice(t * P, (t + 1) * P)
             for j0, n in ((0, HALF), (HALF, HALF)) if t == 0 else ((0, S),):
                 bank = psum.tile([P, S], F32, name="bank")
-                nc.tensor.matmul_mx(
-                    out=bank[:, :n],
-                    lhsT=w1_codes[:, rows].bitcast(FP8X4),
-                    lhsT_scale=w1_scale[:, rows],
-                    rhs=x_codes[:, j0 : j0 + n].bitcast(FP8X4),
-                    rhs_scale=x_scale[:, j0 : j0 + n],
-                    start=True,
-                    stop=True,
-                )
+                product(bank[:, :n], w1_codes, w1_scale, t, x_codes[:, j0 : j0 + n], x_scale[:, j0 : j0 + n])
                 nc.scalar.activation(y_rows[t][:, j0 : j0 + n], bank[:, :n], ACT.Copy, scale=half_gain[:, t : t + 1])
 
         w2_dealt = keep.tile([P, PACK, P, PACK], BF16, align_bytes=64)
@@ -106,85 +118,123 @@ def tile_picked_rangelay_none_p_kernel(tc, x_words, x_scales, w1, gn, w2, offs, 
         w2_scale = keep.tile([P, N], U8, align_bytes=64)
         deal_columns(nc.scalar.copy, w2_dealt, w2_raw, 0, P)
 
-        h_rows = [keep.tile([P, S], F32, name="h_rows%d" % t, align_bytes=64) for t in range(PACK)]
+        h_all = keep.tile([P, PACK, S], F32, align_bytes=64)
         penalty = [keep.tile([P, S], F32, name="penalty%d" % t, align_bytes=64) for t in range(PACK)]
-        positive = [keep.tile([P, S], F32, name="positive%d" % t, align_bytes=64) for t in range(PACK)]
 
         work = {}
-        for c, (j0, n) in enumerate(CHUNKS):
-            for name in ("a", "db", "dc", "hi", "lo"):
-                for t in range(PACK):
-                    work[name, c, t] = keep.tile([P, n], F32, name="%s_%d_%d" % (name, c, t), align_bytes=64)
-            work["z", c] = keep.tile([P, PACK, n], F32, name="z_%d" % c, align_bytes=64)
-            work["zb", c] = keep.tile([P, n, PACK], BF16, name="zb_%d" % c, align_bytes=64)
-            work["zc", c] = keep.tile([P, n], U32, name="zc_%d" % c, align_bytes=64)
-            work["zs", c] = keep.tile([P, n], U8, name="zs_%d" % c, align_bytes=64)
 
-        def fetch_first(c, t):
-            j0, n = CHUNKS[c]
-            nc.vector.tensor_copy(work["a", c, t][:], y_rows[t][:].indirect(entries(lists["n1"], j0, n)))
+        def scratch(name, b, t):
+            work[name, b, t] = keep.tile([P, BLOCK], F32, name="%s_%d_%d" % (name, b, t), align_bytes=64)
+            return work[name, b, t]
 
-        def fetch_differences(c, t):
-            j0, n = CHUNKS[c]
+        def fetch_first(b, t):
+            if t == 0:
+                work["a", b] = keep.tile([P, PACK, BLOCK], F32, name="shared%d" % (b - 2) if b >= 2 else "a%d" % b, align_bytes=64)
+            nc.vector.tensor_copy(work["a", b][:, t, :], y_rows[t][:].indirect(entries(lists["n1"], b * BLOCK, BLOCK)))
+
+        def fetch_differences(b, t):
             for name, which in (("db", "n2"), ("dc", "n3")):
                 nc.vector.tensor_tensor(
-                    work[name, c, t][:], y_rows[t][:].indirect(entries(lists[which], j0, n)), work["a", c, t][:], ALU.subtract
+                    scratch(name, b, t)[:],
+                    y_rows[t][:].indirect(entries(lists[which], b * BLOCK, BLOCK)),
+                    work["a", b][:, t, :],
+                    ALU.subtract,
                 )
 
-        def extremes(c, t):
+        def extremes(b, t):
             for name, op in (("hi", ALU.max), ("lo", ALU.min)):
-                nc.vector.scalar_tensor_tensor(work[name, c, t][:], work["db", c, t][:], 0.0, work["dc", c, t][:], op, op)
+                nc.vector.scalar_tensor_tensor(scratch(name, b, t)[:], work["db", b, t][:], 0.0, work["dc", b, t][:], op, op)
 
-        def spread(c, t):
+        def sum_turned(b, t):
+            if t == 0:
+                work["sum", b] = psum.tile([P, PACK, P], F32, name="bank")
+            for name, factor in (("hi", hi_factor), ("lo", lo_factor)):
+                nc.scalar.activation(scratch(name + "s", b, t)[:], work[name, b, t][:], ACT.Copy, scale=factor[:, t : t + 1])
+            terms = (work["a", b][:, t, :], work["his", b, t][:], work["los", b, t][:])
+            for i, term in enumerate(terms):
+                nc.tensor.matmul(work["sum", b][:, t, :], term, identity[:], start=i == 0, stop=i == len(terms) - 1, is_transpose=True)
+            if t < PACK - 1:
+                return
+            turned = keep.tile([P, 2, P, 2], BF16, name="turned%d" % b, align_bytes=64)
+            nc.scalar.copy(out=turned[:], in_=work["sum", b][:].rearrange("j (u e) p -> j u p e", e=2))
+            pairs = turned[:].rearrange("j u p e -> j u (p e)").bitcast(F32)
+            back = psum.tile([P, 2, BLOCK], F32, name="bank")
+            for u in range(2):
+                nc.tensor.transpose(back[:, u, :], pairs[:, u, :], identity[:])
+            work["zb", b] = keep.tile([P, BLOCK, PACK], BF16, name="shared%d" % b, align_bytes=64)
+            nc.scalar.copy(out=work["zb", b][:].bitcast(F32), in_=back[:].rearrange("p u j -> p j u"))
+
+        def spread(b, t):
             nc.vector.scalar_tensor_tensor(
-                work["db", c, t][:], work["lo", c, t][:], min_share[:, t : t + 1], work["hi", c, t][:], ALU.mult, ALU.add
+                work["db", b, t][:], work["lo", b, t][:], lo_share[:, t : t + 1], work["hi", b, t][:], ALU.mult, ALU.add
             )
 
-        def finish_z(c, t):
+        def finish_z(b, t):
+            if t == 0:
+                work["z", b] = keep.tile([P, PACK, BLOCK], F32, name="z%d" % b, align_bytes=64)
             nc.vector.scalar_tensor_tensor(
-                work["z", c][:, t, :], work["db", c, t][:], range_factor[:, t : t + 1], work["a", c, t][:], ALU.mult, ALU.add
+                work["z", b][:, t, :], work["db", b, t][:], hi_factor[:, t : t + 1], work["a", b][:, t, :], ALU.mult, ALU.add
             )
             if t == PACK - 1:
-                nc.scalar.copy(
-                    out=work["zb", c][:].rearrange("p (g i) t -> p g t i", i=4),
-                    in_=work["z", c][:].rearrange("p t (g i) -> p g t i", i=4),
+                work["zb", b] = keep.tile([P, BLOCK, PACK], BF16, name="zb%d" % b, align_bytes=64)
+                nc.vector.tensor_copy(
+                    out=work["zb", b][:].rearrange("p (g i) t -> p g t i", i=4),
+                    in_=work["z", b][:].rearrange("p t (g i) -> p g t i", i=4),
                 )
 
-        def second_product(c, t):
-            if c == 0 and t == 0:
+        def second_product(b):
+            if b == 0:
                 nc.vector.quantize_mx(w2_codes[:].bitcast(FP8X4), w2_scale[:], w2_dealt[:].rearrange("p t m j -> p (t m j)"))
-            if t != PACK - 1:
-                return
-            j0, n = CHUNKS[c]
-            last = c == len(CHUNKS) - 1
-            nc.vector.quantize_mx(work["zc", c][:].bitcast(FP8X4), work["zs", c][:], work["zb", c][:].rearrange("p n t -> p (n t)"))
-            for u in range(PACK):
-                rows = slice(u * P, (u + 1) * P)
-                bank = psum.tile([P, S], F32, name="bank")
-                nc.tensor.matmul_mx(
-                    out=bank[:, :n],
-                    lhsT=w2_codes[:, rows].bitcast(FP8X4),
-                    lhsT_scale=w2_scale[:, rows],
-                    rhs=work["zc", c][:].bitcast(FP8X4),
-                    rhs_scale=work["zs", c][:],
-                    start=True,
-                    stop=True,
-                )
-                cols = slice(j0, j0 + n)
-                if last and u == 0:
-                    nc.vector.tensor_scalar(penalty[u][:, cols], bank[:, :n], -0.5, 0.0, ALU.mult, ALU.min)
-                    nc.scalar.copy(h_rows[u][:, cols], bank[:, :n])
-                else:
-                    nc.scalar.activation(positive[u][:, cols], bank[:, :n], ACT.Relu, scale=0.5)
-                    nc.scalar.copy(h_rows[u][:, cols], bank[:, :n])
-                    nc.scalar.mul(penalty[u][:, cols], positive[u][:, cols], -1.0)
+            z_codes = keep.tile([P, BLOCK], U32, name="z_codes%d" % b, align_bytes=64)
+            z_scale = keep.tile([P, BLOCK], U8, name="z_scale%d" % b, align_bytes=64)
+            nc.vector.quantize_mx(z_codes[:].bitcast(FP8X4), z_scale[:], work["zb", b][:].rearrange("p n t -> p (n t)"))
+            first = 1 if b == LAST else 0
+            if first:
+                work["h0"] = psum.tile([P, BLOCK], F32, name="bank")
+                product(work["h0"][:], w2_codes, w2_scale, 0, z_codes[:], z_scale[:])
+            work["h", b] = psum.tile([P, PACK - first, BLOCK], F32, name="bank")
+            for u in range(first, PACK):
+                product(work["h", b][:, u - first, :], w2_codes, w2_scale, u, z_codes[:], z_scale[:])
 
-        units = [(c, t) for c in range(len(CHUNKS)) for t in range(PACK)]
-        stages = (fetch_first, fetch_differences, extremes, spread, finish_z, second_product)
-        for step in range(len(units) + len(stages) - 1):
-            for lag, stage in enumerate(stages):
+        def take_h(b):
+            cols = slice(b * BLOCK, (b + 1) * BLOCK)
+            first = 1 if b == LAST else 0
+            if first:
+                nc.vector.tensor_scalar(penalty[0][:, cols], work["h0"][:], -0.5, 0.0, ALU.mult, ALU.min)
+                nc.scalar.copy(h_all[:, 0, cols], work["h0"][:])
+            bank = work["h", b]
+            positive = keep.tile([P, PACK - first, BLOCK], F32, name="positive%d" % b, align_bytes=64)
+            nc.scalar.activation(positive[:], bank[:], ACT.Relu, scale=0.5)
+            nc.scalar.mul(penalty[first][:, cols], positive[:, 0, :], -1.0)
+            nc.scalar.copy(h_all[:, first:, cols], bank[:])
+            for u in range(first + 1, PACK):
+                nc.scalar.mul(penalty[u][:, cols], positive[:, u - first, :], -1.0)
+
+        def combine(b, t):
+            if b < 3:
+                sum_turned(b, t)
+            else:
+                spread(b, t)
+
+        def finish(b, t):
+            if b >= 3:
+                finish_z(b, t)
+
+        def multiply(b, t):
+            if t == PACK - 1:
+                second_product(b)
+
+        def evacuate(b, t):
+            if t == PACK - 1:
+                take_h(b)
+
+        units = [(b, t) for b in range(BLOCKS) for t in range(PACK)]
+        stages = ((0, fetch_first), (1, fetch_differences), (2, extremes), (3, combine), (4, finish), (5, multiply), (8, evacuate))
+        for step in range(len(units) + stages[-1][0]):
+            for lag, stage in stages:
                 if 0 <= step - lag < len(units):
                     stage(*units[step - lag])
+
 
         out_rows = out.rearrange("(p t) s -> p t s", t=PACK)
         for u in range(PACK):
@@ -192,7 +242,7 @@ def tile_picked_rangelay_none_p_kernel(tc, x_words, x_scales, w1, gn, w2, offs, 
             for j0 in (0, HALF):
                 cols = slice(j0, j0 + HALF)
                 nc.vector.tensor_tensor(
-                    result[:, cols], penalty[u][:].indirect(entries(lists["n4"], j0, HALF)), h_rows[u][:, cols], ALU.add
+                    result[:, cols], penalty[u][:].indirect(entries(lists["n4"], j0, HALF)), h_all[:, u, cols], ALU.add
                 )
                 if u == PACK - 1:
                     nc.sync.dma_start(out=out_rows[:, u, cols], in_=result[:, cols])

@@ -18,29 +18,27 @@ ACT = mybir.ActivationFunctionType
 
 P = 128
 PACK = 4
+PAIR = 2
 LIST_ROWS = 16
 HALF = S // 2
-BLOCK = 128
-BLOCKS = S // BLOCK
-LAST = BLOCKS - 1
+CHUNKS = ((0, 256), (256, 128), (384, 128))
+LAST = len(CHUNKS) - 1
 
 
 def entries(list_tile, start, count):
     return list_tile[:, start // LIST_ROWS : (start + count) // LIST_ROWS]
 
 
-def deal_columns(copy, dealt, raw, m0, m1):
-    copy(
-        out=dealt[:, :, m0:m1, :].rearrange("p t m j -> p m j t"),
-        in_=raw[:].rearrange("p j (m t) -> p m j t", t=PACK),
-    )
+def deal_columns(copy, dealt, raw):
+    copy(out=dealt.rearrange("p t m j -> p m j t"), in_=raw.rearrange("p j (m t) -> p m j t", t=PACK))
 
 
 def tile_picked_rangelay_none_p_kernel(tc, x_words, x_scales, w1, gn, w2, offs, n1, n2, n3, n4, out):
     nc = tc.nc
     with ExitStack() as ctx:
         keep = ctx.enter_context(tc.tile_pool(name="keep", bufs=1))
-        psum = ctx.enter_context(tc.psum_pool(name="psum", bufs=8))
+        psum = ctx.enter_context(tc.psum_pool(name="psum", bufs=7))
+        held = ctx.enter_context(tc.psum_pool(name="held", bufs=1))
 
         lists = {}
         for name in ("offs", "n1", "n2", "n3", "n4"):
@@ -87,8 +85,8 @@ def tile_picked_rangelay_none_p_kernel(tc, x_words, x_scales, w1, gn, w2, offs, 
         w1_dealt = keep.tile([P, PACK, P, PACK], BF16, align_bytes=64)
         w1_codes = keep.tile([P, H], U32, align_bytes=64)
         w1_scale = keep.tile([P, H], U8, align_bytes=64)
-        deal_columns(nc.scalar.copy, w1_dealt, w1_raw[0], 0, 64)
-        deal_columns(nc.vector.tensor_copy, w1_dealt, w1_raw[1], 64, P)
+        deal_columns(nc.scalar.copy, w1_dealt[:, :, : P // 2, :], w1_raw[0][:])
+        deal_columns(nc.vector.tensor_copy, w1_dealt[:, :, P // 2 :, :], w1_raw[1][:])
         nc.vector.quantize_mx(w1_codes[:].bitcast(FP8X4), w1_scale[:], w1_dealt[:].rearrange("p t m j -> p (t m j)"))
 
         x_codes = keep.tile([P, S], U32, align_bytes=64)
@@ -114,135 +112,178 @@ def tile_picked_rangelay_none_p_kernel(tc, x_words, x_scales, w1, gn, w2, offs, 
                 nc.scalar.activation(y_rows[t][:, j0 : j0 + n], bank[:, :n], ACT.Copy, scale=half_gain[:, t : t + 1])
 
         w2_dealt = keep.tile([P, PACK, P, PACK], BF16, align_bytes=64)
-        w2_codes = keep.tile([P, N], U32, align_bytes=64)
-        w2_scale = keep.tile([P, N], U8, align_bytes=64)
-        deal_columns(nc.scalar.copy, w2_dealt, w2_raw, 0, P)
+        deal_columns(nc.scalar.copy, w2_dealt[:], w2_raw[:])
 
         h_all = keep.tile([P, PACK, S], F32, align_bytes=64)
-        penalty = [keep.tile([P, S], F32, name="penalty%d" % t, align_bytes=64) for t in range(PACK)]
+        penalty = [keep.tile([P, S], F32, name="penalty%d" % u, align_bytes=64) for u in range(PACK)]
 
         work = {}
+        after = {
+            ("a", 2, 0): ("z_bf16", 0, 0),
+            ("diff", 2, 1): ("z_bf16", 1, 0),
+            ("z_codes", 1, 0): ("diff", 2, 0),
+            ("w2_codes", 1, 0): ("hi", 2, 3),
+            ("scaled", 1, 0): ("turned", 0, 1),
+            ("scaled", 2, 0): ("turned", 1, 0),
+        }
 
-        def scratch(name, b, t):
-            work[name, b, t] = keep.tile([P, BLOCK], F32, name="%s_%d_%d" % (name, b, t), align_bytes=64)
-            return work[name, b, t]
+        def scratch(key, shape, dtype):
+            work[key] = keep.tile(shape, dtype, name="%s_%d_%d" % after.get(key, key), align_bytes=64)
+            return work[key]
 
-        def fetch_first(b, t):
+        def quantize_w2(pair):
+            codes = scratch(("w2_codes", pair, 0), [P, PAIR * P], U32)
+            scale = scratch(("w2_scale", pair, 0), [P, PAIR * P], U8)
+            dealt = w2_dealt[:, PAIR * pair : PAIR * (pair + 1), :, :].rearrange("p t m j -> p (t m j)")
+            nc.vector.quantize_mx(codes[:].bitcast(FP8X4), scale[:], dealt)
+
+        def h_product(bank_cols, u, c):
+            pair = u // PAIR
+            product(
+                bank_cols, work["w2_codes", pair, 0], work["w2_scale", pair, 0], u % PAIR,
+                work["z_codes", c, 0][:], work["z_scale", c, 0][:],
+            )
+
+        def fetch_first(c, t):
+            j0, n = CHUNKS[c]
             if t == 0:
-                work["a", b] = keep.tile([P, PACK, BLOCK], F32, name="shared%d" % (b - 2) if b >= 2 else "a%d" % b, align_bytes=64)
-            nc.vector.tensor_copy(work["a", b][:, t, :], y_rows[t][:].indirect(entries(lists["n1"], b * BLOCK, BLOCK)))
+                scratch(("a", c, 0), [P, PACK, n], F32)
+            nc.vector.tensor_copy(work["a", c, 0][:, t, :], y_rows[t][:].indirect(entries(lists["n1"], j0, n)))
 
-        def fetch_differences(b, t):
-            for name, which in (("db", "n2"), ("dc", "n3")):
+        def fetch_differences(c, t):
+            j0, n = CHUNKS[c]
+            if t % PAIR == 0:
+                scratch(("diff", c, t // PAIR), [P, PAIR, 2, n], F32)
+            for i, (name, which) in enumerate((("db", "n2"), ("dc", "n3"))):
+                work[name, c, t] = work["diff", c, t // PAIR][:, t % PAIR, i, :]
                 nc.vector.tensor_tensor(
-                    scratch(name, b, t)[:],
-                    y_rows[t][:].indirect(entries(lists[which], b * BLOCK, BLOCK)),
-                    work["a", b][:, t, :],
+                    work[name, c, t],
+                    y_rows[t][:].indirect(entries(lists[which], j0, n)),
+                    work["a", c, 0][:, t, :],
                     ALU.subtract,
                 )
 
-        def extremes(b, t):
+        def extremes(c, t):
+            n = CHUNKS[c][1]
             for name, op in (("hi", ALU.max), ("lo", ALU.min)):
-                nc.vector.scalar_tensor_tensor(scratch(name, b, t)[:], work["db", b, t][:], 0.0, work["dc", b, t][:], op, op)
-
-        def sum_turned(b, t):
-            if t == 0:
-                work["sum", b] = psum.tile([P, PACK, P], F32, name="bank")
-            for name, factor in (("hi", hi_factor), ("lo", lo_factor)):
-                nc.scalar.activation(scratch(name + "s", b, t)[:], work[name, b, t][:], ACT.Copy, scale=factor[:, t : t + 1])
-            terms = (work["a", b][:, t, :], work["his", b, t][:], work["los", b, t][:])
-            for i, term in enumerate(terms):
-                nc.tensor.matmul(work["sum", b][:, t, :], term, identity[:], start=i == 0, stop=i == len(terms) - 1, is_transpose=True)
-            if t < PACK - 1:
-                return
-            turned = keep.tile([P, 2, P, 2], BF16, name="turned%d" % b, align_bytes=64)
-            nc.scalar.copy(out=turned[:], in_=work["sum", b][:].rearrange("j (u e) p -> j u p e", e=2))
-            pairs = turned[:].rearrange("j u p e -> j u (p e)").bitcast(F32)
-            back = psum.tile([P, 2, BLOCK], F32, name="bank")
-            for u in range(2):
-                nc.tensor.transpose(back[:, u, :], pairs[:, u, :], identity[:])
-            work["zb", b] = keep.tile([P, BLOCK, PACK], BF16, name="shared%d" % b, align_bytes=64)
-            nc.scalar.copy(out=work["zb", b][:].bitcast(F32), in_=back[:].rearrange("p u j -> p j u"))
-
-        def spread(b, t):
-            nc.vector.scalar_tensor_tensor(
-                work["db", b, t][:], work["lo", b, t][:], lo_share[:, t : t + 1], work["hi", b, t][:], ALU.mult, ALU.add
-            )
-
-        def finish_z(b, t):
-            if t == 0:
-                work["z", b] = keep.tile([P, PACK, BLOCK], F32, name="z%d" % b, align_bytes=64)
-            nc.vector.scalar_tensor_tensor(
-                work["z", b][:, t, :], work["db", b, t][:], hi_factor[:, t : t + 1], work["a", b][:, t, :], ALU.mult, ALU.add
-            )
-            if t == PACK - 1:
-                work["zb", b] = keep.tile([P, BLOCK, PACK], BF16, name="zb%d" % b, align_bytes=64)
-                nc.vector.tensor_copy(
-                    out=work["zb", b][:].rearrange("p (g i) t -> p g t i", i=4),
-                    in_=work["z", b][:].rearrange("p t (g i) -> p g t i", i=4),
+                nc.vector.scalar_tensor_tensor(
+                    scratch((name, c, t), [P, n], F32)[:], work["db", c, t], 0.0, work["dc", c, t], op, op
                 )
 
-        def second_product(b):
-            if b == 0:
-                nc.vector.quantize_mx(w2_codes[:].bitcast(FP8X4), w2_scale[:], w2_dealt[:].rearrange("p t m j -> p (t m j)"))
-            z_codes = keep.tile([P, BLOCK], U32, name="z_codes%d" % b, align_bytes=64)
-            z_scale = keep.tile([P, BLOCK], U8, name="z_scale%d" % b, align_bytes=64)
-            nc.vector.quantize_mx(z_codes[:].bitcast(FP8X4), z_scale[:], work["zb", b][:].rearrange("p n t -> p (n t)"))
-            first = 1 if b == LAST else 0
-            if first:
-                work["h0"] = psum.tile([P, BLOCK], F32, name="bank")
-                product(work["h0"][:], w2_codes, w2_scale, 0, z_codes[:], z_scale[:])
-            work["h", b] = psum.tile([P, PACK - first, BLOCK], F32, name="bank")
-            for u in range(first, PACK):
-                product(work["h", b][:, u - first, :], w2_codes, w2_scale, u, z_codes[:], z_scale[:])
+        def sum_turned(c, t):
+            n = CHUNKS[c][1]
+            pairs = 1 if c == LAST else PACK // PAIR
+            if t == 0:
+                scratch(("scaled", c, 0), [P, pairs * PAIR, 2, n], F32)
+                scratch(("z_bf16", c, 0), [P, n, PACK], BF16)
+            scaled = work["scaled", c, 0]
+            for i, (name, factor) in enumerate((("hi", hi_factor), ("lo", lo_factor))):
+                nc.scalar.activation(scaled[:, t, i, :], work[name, c, t][:], ACT.Copy, scale=factor[:, t : t + 1])
+            for b in range(n // P):
+                cols = slice(b * P, (b + 1) * P)
+                if t == 0:
+                    work["sum", c, b] = (held if c == 1 else psum).tile([P, pairs * PAIR, P], F32, name="bank")
+                terms = (work["a", c, 0][:, t, cols], scaled[:, t, 0, cols], scaled[:, t, 1, cols])
+                for i, term in enumerate(terms):
+                    nc.tensor.matmul(
+                        work["sum", c, b][:, t, :], term, identity[:], start=i == 0, stop=i == len(terms) - 1, is_transpose=True
+                    )
+            if t < pairs * PAIR - 1:
+                return
+            for b in range(n // P):
+                turned = scratch(("turned", c, b), [P, pairs, P, PAIR], BF16)
+                nc.scalar.copy(out=turned[:], in_=work["sum", c, b][:].rearrange("j (u e) p -> j u p e", e=PAIR))
+                words = turned[:].rearrange("j u p e -> j u (p e)").bitcast(F32)
+                work["back", c, b] = psum.tile([P, pairs, P], F32, name="bank")
+                for u in range(pairs):
+                    nc.tensor.transpose(work["back", c, b][:, u, :], words[:, u, :], identity[:])
+            for b in range(n // P):
+                z_words = work["z_bf16", c, 0][:, b * P : (b + 1) * P, :].bitcast(F32)
+                nc.scalar.copy(out=z_words[:, :, :pairs], in_=work["back", c, b][:].rearrange("p u j -> p j u"))
 
-        def take_h(b):
-            cols = slice(b * BLOCK, (b + 1) * BLOCK)
-            first = 1 if b == LAST else 0
-            if first:
-                nc.vector.tensor_scalar(penalty[0][:, cols], work["h0"][:], -0.5, 0.0, ALU.mult, ALU.min)
-                nc.scalar.copy(h_all[:, 0, cols], work["h0"][:])
-            bank = work["h", b]
-            positive = keep.tile([P, PACK - first, BLOCK], F32, name="positive%d" % b, align_bytes=64)
-            nc.scalar.activation(positive[:], bank[:], ACT.Relu, scale=0.5)
-            nc.scalar.mul(penalty[first][:, cols], positive[:, 0, :], -1.0)
-            nc.scalar.copy(h_all[:, first:, cols], bank[:])
-            for u in range(first + 1, PACK):
-                nc.scalar.mul(penalty[u][:, cols], positive[:, u - first, :], -1.0)
+        def on_vector(c, t):
+            return c == LAST and t >= PAIR
 
-        def combine(b, t):
-            if b < 3:
-                sum_turned(b, t)
-            else:
-                spread(b, t)
+        def combine(c, t):
+            if not on_vector(c, t):
+                sum_turned(c, t)
+                return
+            nc.vector.scalar_tensor_tensor(
+                work["db", c, t], work["lo", c, t][:], lo_share[:, t : t + 1], work["hi", c, t][:], ALU.mult, ALU.add
+            )
 
-        def finish(b, t):
-            if b >= 3:
-                finish_z(b, t)
-
-        def multiply(b, t):
+        def finish(c, t):
+            if not on_vector(c, t):
+                return
+            n = CHUNKS[c][1]
+            if t == PAIR:
+                scratch(("z_f32", c, 0), [P, PAIR, n], F32)
+            z_f32 = work["z_f32", c, 0]
+            nc.vector.scalar_tensor_tensor(
+                z_f32[:, t - PAIR, :], work["db", c, t], hi_factor[:, t : t + 1], work["a", c, 0][:, t, :], ALU.mult, ALU.add
+            )
             if t == PACK - 1:
-                second_product(b)
+                nc.vector.tensor_copy(out=work["z_bf16", c, 0][:, :, PAIR:], in_=z_f32[:].rearrange("p e j -> p j e"))
 
-        def evacuate(b, t):
-            if t == PACK - 1:
-                take_h(b)
+        def multiply(c, t):
+            if t < PACK - 1:
+                return
+            n = CHUNKS[c][1]
+            if c == 0:
+                quantize_w2(0)
+            z_codes = scratch(("z_codes", c, 0), [P, n], U32)
+            z_scale = scratch(("z_scale", c, 0), [P, n], U8)
+            nc.vector.quantize_mx(z_codes[:].bitcast(FP8X4), z_scale[:], work["z_bf16", c, 0][:].rearrange("p n t -> p (n t)"))
 
-        units = [(b, t) for b in range(BLOCKS) for t in range(PACK)]
-        stages = ((0, fetch_first), (1, fetch_differences), (2, extremes), (3, combine), (4, finish), (5, multiply), (8, evacuate))
+        def take_rows(u, cols, bank_cols):
+            positive = scratch(("positive", u, cols.start), [P, cols.stop - cols.start], F32)
+            nc.scalar.activation(positive[:], bank_cols, ACT.Relu, scale=0.5)
+            nc.scalar.mul(penalty[u][:, cols], positive[:], -1.0)
+            nc.scalar.copy(h_all[:, u, cols], bank_cols)
+
+        def evacuate(c, t):
+            if t < PACK - 1:
+                return
+            j0, n = CHUNKS[c]
+            cols = slice(j0, j0 + n)
+            if c == LAST:
+                for u in range(PAIR):
+                    work["h", c, u] = psum.tile([P, n], F32, name="bank")
+                    h_product(work["h", c, u][:], u, c)
+                nc.vector.tensor_scalar(penalty[0][:, cols], work["h", c, 0][:], -0.5, 0.0, ALU.mult, ALU.min)
+                nc.scalar.copy(h_all[:, 0, cols], work["h", c, 0][:])
+                take_rows(1, cols, work["h", c, 1][:])
+                return
+            work["h", c] = (held if c == 0 else psum).tile([P, PAIR, n], F32, name="bank")
+            for u in range(PAIR):
+                h_product(work["h", c][:, u, :], u, c)
+            positive = scratch(("positive_pair", c, 0), [P, PAIR, n], F32)
+            nc.scalar.activation(positive[:], work["h", c][:], ACT.Relu, scale=0.5)
+            nc.scalar.copy(h_all[:, :PAIR, cols], work["h", c][:])
+            for u in range(PAIR):
+                nc.scalar.mul(penalty[u][:, cols], positive[:, u, :], -1.0)
+
+        units = [(c, t) for c in range(len(CHUNKS)) for t in range(PACK)]
+        stages = ((5, multiply), (0, fetch_first), (1, fetch_differences), (2, extremes), (3, combine), (4, finish), (9, evacuate))
         for step in range(len(units) + stages[-1][0]):
             for lag, stage in stages:
                 if 0 <= step - lag < len(units):
                     stage(*units[step - lag])
 
+        quantize_w2(1)
+        for u in range(PAIR, PACK):
+            bank = psum.tile([P, S], F32, name="bank")
+            for c, (j0, n) in enumerate(CHUNKS):
+                h_product(bank[:, j0 : j0 + n], u, c)
+            take_rows(u, slice(0, S), bank[:])
 
         out_rows = out.rearrange("(p t) s -> p t s", t=PACK)
         for u in range(PACK):
             result = keep.tile([P, S], F32, name="result%d" % u, align_bytes=64)
-            for j0 in (0, HALF):
-                cols = slice(j0, j0 + HALF)
+            for j0, n in CHUNKS if u == PACK - 1 else ((0, HALF), (HALF, HALF)):
+                cols = slice(j0, j0 + n)
                 nc.vector.tensor_tensor(
-                    result[:, cols], penalty[u][:].indirect(entries(lists["n4"], j0, HALF)), h_all[:, u, cols], ALU.add
+                    result[:, cols], penalty[u][:].indirect(entries(lists["n4"], j0, n)), h_all[:, u, cols], ALU.add
                 )
                 if u == PACK - 1:
                     nc.sync.dma_start(out=out_rows[:, u, cols], in_=result[:, cols])

from contextlib import ExitStack

import concourse.mybir as mybir
from concourse.masks import make_identity

K, T, S, N, H = 512, 2048, 512, 512, 512
FLOPS = 2 * K * H * S + 2 * H * N * S

F32 = mybir.dt.float32
BF16 = mybir.dt.bfloat16
I32 = mybir.dt.int32
U32 = mybir.dt.uint32
U16 = mybir.dt.uint16
U8 = mybir.dt.uint8
FP8X4 = mybir.dt.float8_e4m3fn_x4
ALU = mybir.AluOpType
ACT = mybir.ActivationFunctionType

P = 128
PACK = 4
PAIR = 2
LIST_ROWS = 16
HALF = S // 2
CHUNKS = ((0, 256), (256, 128), (384, 128))
LAST = len(CHUNKS) - 1


def entries(list_tile, start, count):
    return list_tile[:, start // LIST_ROWS : (start + count) // LIST_ROWS]


def deal_columns(copy, dealt, raw):
    copy(out=dealt.rearrange("p t m j -> p m j t"), in_=raw.rearrange("p j (m t) -> p m j t", t=PACK))


def tile_picked_rangelay_none_p_kernel(tc, x_words, x_scales, w1, gn, w2, offs, n1, n2, n3, n4, out):
    nc = tc.nc
    with ExitStack() as ctx:
        keep = ctx.enter_context(tc.tile_pool(name="keep", bufs=1))
        psum = ctx.enter_context(tc.psum_pool(name="psum", bufs=7))
        held = ctx.enter_context(tc.psum_pool(name="held", bufs=1))

        lists = {}
        for name in ("offs", "n1", "n2", "n3", "n4"):
            lists[name] = keep.tile([P, S // LIST_ROWS], U16, name="list_" + name)
        all_words = keep.tile([P, T], U32, align_bytes=64)
        all_scales = keep.tile([P, T], U8, align_bytes=64)
        w1_raw = [keep.tile([P, PACK, H // 2], F32, name="w1_raw%d" % i, align_bytes=64) for i in range(2)]
        w1_rows = w1.rearrange("(p j) c -> p j c", j=PACK)
        w2_raw = keep.tile([P, PACK, N], F32, align_bytes=64)
        gain = keep.tile([P, PACK], F32)

        nc.vector.memset(all_scales[:].bitcast(I32), 0)
        nc.scalar.dma_start(out=gain[:], in_=gn.rearrange("(p t) o -> p (t o)", t=PACK))
        nc.sync.dma_start(out=w1_raw[0][:], in_=w1_rows[:, :, : H // 2])
        for q in range(4):
            nc.sync.dma_start(
                out=all_scales[32 * q : 32 * q + 4, :].bitcast(I32), in_=x_scales[0, 4 * q : 4 * q + 4, :].bitcast(I32)
            )
        nc.sync.dma_start(lists["offs"][:], offs)
        nc.sync.dma_start(out=w1_raw[1][:], in_=w1_rows[:, :, H // 2 :])
        nc.sync.dma_start(out=all_words[:].bitcast(I32), in_=x_words[0].rearrange("p n t -> p (n t)").bitcast(I32))
        nc.sync.dma_start(lists["n1"][:], n1)
        nc.sync.dma_start(lists["n2"][:], n2)
        nc.sync.dma_start(lists["n3"][:], n3)
        nc.sync.dma_start(out=w2_raw[:], in_=w2.rearrange("(p j) c -> p j c", j=PACK))
        nc.sync.dma_start(lists["n4"][:], n4)

        identity = keep.tile([P, P], F32, align_bytes=64)
        make_identity(nc, identity[:])

        half_gain = keep.tile([P, PACK], F32)
        not_negative = keep.tile([P, PACK], F32)
        hi_factor = keep.tile([P, PACK], F32)
        lo_factor = keep.tile([P, PACK], F32)
        lo_share = keep.tile([P, PACK], F32)
        nc.vector.tensor_scalar(not_negative[:], gain[:], 0.0, None, ALU.is_ge)
        nc.scalar.activation(half_gain[:], gain[:], ACT.Copy, scale=0.5)
        x_scale = keep.tile([P, S], U8, align_bytes=64)
        nc.vector.tensor_copy(x_scale[:], all_scales[:].indirect(lists["offs"][:]))
        nc.vector.tensor_scalar(hi_factor[:], not_negative[:], 3.0, -1.0, ALU.mult, ALU.add)
        nc.vector.tensor_scalar(lo_factor[:], not_negative[:], -3.0, 2.0, ALU.mult, ALU.add)
        nc.vector.tensor_scalar(lo_share[:], not_negative[:], 1.5, -2.0, ALU.mult, ALU.add)

        w1_dealt = keep.tile([P, PACK, P, PACK], BF16, align_bytes=64)
        w1_codes = keep.tile([P, H], U32, align_bytes=64)
        w1_scale = keep.tile([P, H], U8, align_bytes=64)
        deal_columns(nc.scalar.copy, w1_dealt[:, :, : P // 2, :], w1_raw[0][:])
        deal_columns(nc.vector.tensor_copy, w1_dealt[:, :, P // 2 :, :], w1_raw[1][:])
        nc.vector.quantize_mx(w1_codes[:].bitcast(FP8X4), w1_scale[:], w1_dealt[:].rearrange("p t m j -> p (t m j)"))

        x_codes = keep.tile([P, S], U32, align_bytes=64)
        for j0 in (0, HALF):
            nc.vector.tensor_copy(x_codes[:, j0 : j0 + HALF], all_words[:].indirect(entries(lists["offs"], j0, HALF)))

        def product(bank_cols, codes, scale, rows, moving_codes, moving_scale):
            nc.tensor.matmul_mx(
                out=bank_cols,
                lhsT=codes[:, rows * P : (rows + 1) * P].bitcast(FP8X4),
                lhsT_scale=scale[:, rows * P : (rows + 1) * P],
                rhs=moving_codes.bitcast(FP8X4),
                rhs_scale=moving_scale,
                start=True,
                stop=True,
            )

        y_rows = [keep.tile([P, S], F32, name="y_rows%d" % t, align_bytes=64) for t in range(PACK)]
        for t in range(PACK):
            for j0, n in ((0, HALF), (HALF, HALF)) if t == 0 else ((0, S),):
                bank = psum.tile([P, S], F32, name="bank")
                product(bank[:, :n], w1_codes, w1_scale, t, x_codes[:, j0 : j0 + n], x_scale[:, j0 : j0 + n])
                nc.scalar.activation(y_rows[t][:, j0 : j0 + n], bank[:, :n], ACT.Copy, scale=half_gain[:, t : t + 1])

        w2_dealt = keep.tile([P, PACK, P, PACK], BF16, align_bytes=64)
        deal_columns(nc.scalar.copy, w2_dealt[:], w2_raw[:])

        h_all = keep.tile([P, PACK, S], F32, align_bytes=64)
        penalty = [keep.tile([P, S], F32, name="penalty%d" % u, align_bytes=64) for u in range(PACK)]

        work = {}
        after = {
            ("a", 2, 0): ("z_bf16", 0, 0),
            ("diff", 2, 1): ("z_bf16", 1, 0),
            ("z_codes", 1, 0): ("diff", 2, 0),
            ("w2_codes", 1, 0): ("hi", 2, 3),
            ("scaled", 1, 0): ("turned", 0, 1),
            ("scaled", 2, 0): ("turned", 1, 0),
        }

        def scratch(key, shape, dtype):
            work[key] = keep.tile(shape, dtype, name="%s_%d_%d" % after.get(key, key), align_bytes=64)
            return work[key]

        def quantize_w2(pair):
            codes = scratch(("w2_codes", pair, 0), [P, PAIR * P], U32)
            scale = scratch(("w2_scale", pair, 0), [P, PAIR * P], U8)
            dealt = w2_dealt[:, PAIR * pair : PAIR * (pair + 1), :, :].rearrange("p t m j -> p (t m j)")
            nc.vector.quantize_mx(codes[:].bitcast(FP8X4), scale[:], dealt)

        def h_product(bank_cols, u, c):
            pair = u // PAIR
            product(
                bank_cols, work["w2_codes", pair, 0], work["w2_scale", pair, 0], u % PAIR,
                work["z_codes", c, 0][:], work["z_scale", c, 0][:],
            )

        def fetch_first(c, t):
            j0, n = CHUNKS[c]
            if t == 0:
                scratch(("a", c, 0), [P, PACK, n], F32)
            nc.vector.tensor_copy(work["a", c, 0][:, t, :], y_rows[t][:].indirect(entries(lists["n1"], j0, n)))

        def fetch_differences(c, t):
            j0, n = CHUNKS[c]
            if t % PAIR == 0:
                scratch(("diff", c, t // PAIR), [P, PAIR, 2, n], F32)
            for i, (name, which) in enumerate((("db", "n2"), ("dc", "n3"))):
                work[name, c, t] = work["diff", c, t // PAIR][:, t % PAIR, i, :]
                nc.vector.tensor_tensor(
                    work[name, c, t],
                    y_rows[t][:].indirect(entries(lists[which], j0, n)),
                    work["a", c, 0][:, t, :],
                    ALU.subtract,
                )

        def extremes(c, t):
            n = CHUNKS[c][1]
            for name, op in (("hi", ALU.max), ("lo", ALU.min)):
                nc.vector.scalar_tensor_tensor(
                    scratch((name, c, t), [P, n], F32)[:], work["db", c, t], 0.0, work["dc", c, t], op, op
                )

        def sum_turned(c, t):
            n = CHUNKS[c][1]
            pairs = 1 if c == LAST else PACK // PAIR
            if t == 0:
                scratch(("scaled", c, 0), [P, pairs * PAIR, 2, n], F32)
                scratch(("z_bf16", c, 0), [P, n, PACK], BF16)
            scaled = work["scaled", c, 0]
            for i, (name, factor) in enumerate((("hi", hi_factor), ("lo", lo_factor))):
                nc.scalar.activation(scaled[:, t, i, :], work[name, c, t][:], ACT.Copy, scale=factor[:, t : t + 1])
            for b in range(n // P):
                cols = slice(b * P, (b + 1) * P)
                if t == 0:
                    work["sum", c, b] = (held if c == 1 else psum).tile([P, pairs * PAIR, P], F32, name="bank")
                terms = (work["a", c, 0][:, t, cols], scaled[:, t, 0, cols], scaled[:, t, 1, cols])
                for i, term in enumerate(terms):
                    nc.tensor.matmul(
                        work["sum", c, b][:, t, :], term, identity[:], start=i == 0, stop=i == len(terms) - 1, is_transpose=True
                    )
            if t < pairs * PAIR - 1:
                return
            for b in range(n // P):
                turned = scratch(("turned", c, b), [P, pairs, P, PAIR], BF16)
                nc.scalar.copy(out=turned[:], in_=work["sum", c, b][:].rearrange("j (u e) p -> j u p e", e=PAIR))
                words = turned[:].rearrange("j u p e -> j u (p e)").bitcast(F32)
                work["back", c, b] = psum.tile([P, pairs, P], F32, name="bank")
                for u in range(pairs):
                    nc.tensor.transpose(work["back", c, b][:, u, :], words[:, u, :], identity[:])
            for b in range(n // P):
                z_words = work["z_bf16", c, 0][:, b * P : (b + 1) * P, :].bitcast(F32)
                nc.scalar.copy(out=z_words[:, :, :pairs], in_=work["back", c, b][:].rearrange("p u j -> p j u"))

        def on_vector(c, t):
            return c == LAST and t >= PAIR

        def combine(c, t):
            if not on_vector(c, t):
                sum_turned(c, t)
                return
            nc.vector.scalar_tensor_tensor(
                work["db", c, t], work["lo", c, t][:], lo_share[:, t : t + 1], work["hi", c, t][:], ALU.mult, ALU.add
            )

        def finish(c, t):
            if not on_vector(c, t):
                return
            n = CHUNKS[c][1]
            if t == PAIR:
                scratch(("z_f32", c, 0), [P, PAIR, n], F32)
            z_f32 = work["z_f32", c, 0]
            nc.vector.scalar_tensor_tensor(
                z_f32[:, t - PAIR, :], work["db", c, t], hi_factor[:, t : t + 1], work["a", c, 0][:, t, :], ALU.mult, ALU.add
            )
            if t == PACK - 1:
                nc.vector.tensor_copy(out=work["z_bf16", c, 0][:, :, PAIR:], in_=z_f32[:].rearrange("p e j -> p j e"))

        def multiply(c, t):
            if t < PACK - 1:
                return
            n = CHUNKS[c][1]
            if c == 0:
                quantize_w2(0)
            z_codes = scratch(("z_codes", c, 0), [P, n], U32)
            z_scale = scratch(("z_scale", c, 0), [P, n], U8)
            nc.vector.quantize_mx(z_codes[:].bitcast(FP8X4), z_scale[:], work["z_bf16", c, 0][:].rearrange("p n t -> p (n t)"))

        def take_rows(u, cols, bank_cols):
            positive = scratch(("positive", u, cols.start), [P, cols.stop - cols.start], F32)
            nc.scalar.activation(positive[:], bank_cols, ACT.Relu, scale=0.5)
            nc.scalar.mul(penalty[u][:, cols], positive[:], -1.0)
            nc.scalar.copy(h_all[:, u, cols], bank_cols)

        def evacuate(c, t):
            if t < PACK - 1:
                return
            j0, n = CHUNKS[c]
            cols = slice(j0, j0 + n)
            if c == LAST:
                for u in range(PAIR):
                    work["h", c, u] = psum.tile([P, n], F32, name="bank")
                    h_product(work["h", c, u][:], u, c)
                nc.vector.tensor_scalar(penalty[0][:, cols], work["h", c, 0][:], -0.5, 0.0, ALU.mult, ALU.min)
                nc.scalar.copy(h_all[:, 0, cols], work["h", c, 0][:])
                take_rows(1, cols, work["h", c, 1][:])
                return
            work["h", c] = (held if c == 0 else psum).tile([P, PAIR, n], F32, name="bank")
            for u in range(PAIR):
                h_product(work["h", c][:, u, :], u, c)
            positive = scratch(("positive_pair", c, 0), [P, PAIR, n], F32)
            nc.scalar.activation(positive[:], work["h", c][:], ACT.Relu, scale=0.5)
            nc.scalar.copy(h_all[:, :PAIR, cols], work["h", c][:])
            for u in range(PAIR):
                nc.scalar.mul(penalty[u][:, cols], positive[:, u, :], -1.0)

        units = [(c, t) for c in range(len(CHUNKS)) for t in range(PACK)]
        stages = ((5, multiply), (0, fetch_first), (1, fetch_differences), (2, extremes), (3, combine), (4, finish), (9, evacuate))
        for step in range(len(units) + stages[-1][0]):
            for lag, stage in stages:
                if 0 <= step - lag < len(units):
                    stage(*units[step - lag])

        quantize_w2(1)
        for u in range(PAIR, PACK):
            bank = psum.tile([P, S], F32, name="bank")
            for c, (j0, n) in enumerate(CHUNKS):
                h_product(bank[:, j0 : j0 + n], u, c)
            take_rows(u, slice(0, S), bank[:])

        out_rows = out.rearrange("(p t) s -> p t s", t=PACK)
        for u in range(PACK):
            result = keep.tile([P, S], F32, name="result%d" % u, align_bytes=64)
            for j0, n in CHUNKS if u == PACK - 1 else ((0, HALF), (HALF, HALF)):
                cols = slice(j0, j0 + n)
                nc.vector.tensor_tensor(
                    result[:, cols], penalty[u][:].indirect(entries(lists["n4"], j0, n)), h_all[:, u, cols], ALU.add
                )
                if u == PACK - 1:
                    nc.sync.dma_start(out=out_rows[:, u, cols], in_=result[:, cols])
            if u < PACK - 1:
                nc.sync.dma_start(out=out_rows[:, u, :], in_=result[:])
